import numpy as np
import ml_dtypes


def mxq(x, axis, fmt="e4m3"):
    dtype, down = {"e4m3": (ml_dtypes.float8_e4m3fn, 7), "e5m2": (ml_dtypes.float8_e5m2, 14)}[fmt]
    v = np.moveaxis(np.asarray(x, np.float32).astype(ml_dtypes.bfloat16).astype(np.float64), axis, -1)
    blocks = v.reshape(v.shape[:-1] + (-1, 32))
    amax = np.abs(blocks).max(-1, keepdims=True)
    byte = np.maximum(np.where(amax > 0, np.frexp(amax)[1] - 1 + 127, 0) - down, 1)
    scale = np.exp2(byte - 127.0)
    codes = (blocks / scale).astype(np.float32).astype(dtype).astype(np.float64)
    return np.moveaxis((codes * scale).reshape(v.shape), -1, axis)


WIDE = False


def mx_kscale(k):
    if not WIDE:
        return np.ones(k)
    levels = np.array([10, -10, 5, -5, 0])
    if k % 512:
        return np.exp2(np.random.permutation(np.resize(levels, k // 32))).repeat(32)
    a = np.empty((k // 512, 16))
    for p in range(k // 512):
        a[p, :8] = np.random.permutation(np.resize(levels, 8))
        for g in range(8):
            far = levels[np.abs(levels - a[p, g]) >= 10]
            a[p, g + 8] = far[np.random.randint(len(far))]
    return np.exp2(a.ravel()).repeat(32)


def f64(x):
    return np.asarray(x).astype(np.float64)


def striped8(idx):
    return np.asarray(idx).reshape(8, -1, 16).transpose(0, 2, 1).reshape(128, -1).astype(np.uint16)


def unstriped8(offs):
    return offs.reshape(8, 16, -1).transpose(0, 2, 1).reshape(8, -1).astype(np.int64)


def pick8(x, idx, run):
    r = np.arange(len(x))
    return x[r[:, None], idx[r % (8 * run) // run]]


E2M1 = np.array([0.0, 0.5, 1.0, 1.5, 2.0, 3.0, 4.0, 6.0, -0.0, -0.5, -1.0, -1.5, -2.0, -3.0, -4.0, -6.0])


def pack_weight(w, fmt):
    k, n = w.shape
    w = f64(np.asarray(w, np.float32).astype(ml_dtypes.bfloat16)).reshape(k // 32, 32, n)
    amax = np.abs(w).max(1)
    if fmt == "e4m3":
        byte = np.frexp(amax)[1] - 1 + 127 - 7
    else:
        mant, ex = np.frexp(amax / 6.0)
        byte = np.where(mant > 0.5, ex, ex - 1) + 127
    byte = np.clip(np.where(amax > 0, byte, 1), 1, 254)
    scaled = (w * np.exp2(127.0 - byte)[:, None, :]).reshape(k, n).astype(np.float32)
    by_word = np.ascontiguousarray(scaled.reshape(k // 512, 128, 4, n).transpose(0, 1, 3, 2))
    if fmt == "e4m3":
        words = by_word.astype(ml_dtypes.float8_e4m3fn).view(np.uint8)
    else:
        c = by_word.astype(ml_dtypes.float4_e2m1fn).view(np.uint8) & 0xF
        words = (c[..., 0::2] | (c[..., 1::2] << 4)).reshape(k // 512, 128, 2 * n)
    return np.ascontiguousarray(words), np.ascontiguousarray(byte.astype(np.uint8).reshape(k // 512, 16, n))


def unpack_weight(words, scales, fmt):
    g, _, n = scales.shape
    words = np.ascontiguousarray(words).reshape(g, 128, n, -1)
    if fmt == "e4m3":
        vals = words.view(ml_dtypes.float8_e4m3fn).astype(np.float64)
    else:
        nib = np.empty((g, 128, n, 4), np.uint8)
        nib[..., 0::2] = words & 0xF
        nib[..., 1::2] = words >> 4
        vals = E2M1[nib]
    vals = vals * np.repeat(np.exp2(scales.astype(np.float64) - 127.0), 8, axis=1)[..., None]
    return vals.transpose(0, 1, 3, 2).reshape(g * 512, n)


D, K, T, U, I, Q = 512, 512, 1024, 1024, 512, 128


def setup_inputs():
    n = np.random.standard_normal
    idx = np.stack([np.random.permutation(U)[:I] for _ in range(8)])
    idx2 = np.stack([np.random.permutation(U)[:I] for _ in range(8)])
    idx3 = np.stack([np.random.permutation(U)[:I] for _ in range(8)])
    idx4 = np.stack([np.random.permutation(T)[:I] for _ in range(8)])
    idx5 = np.stack([np.random.permutation(U)[:I] for _ in range(8)])
    fd = mx_kscale(D)
    fk = mx_kscale(K)
    wqp = pack_weight(n((D, K)) * 1.0 / np.sqrt(D) * fd[:, None] * fk, "e4m3")
    cachep = pack_weight(n((K, T)) * 1.0 / np.sqrt(K) / fk[:, None], "e2m1")
    draftp = pack_weight(n((D, U)) * 1.0 / np.sqrt(D) * fd[:, None], "e4m3")
    return {
        "states": (n((D, Q)) * 0.95 / fd[:, None]).astype(np.float32),
        "wq_words": wqp[0],
        "wq_scales": wqp[1],
        "cache_words": cachep[0],
        "cache_scales": cachep[1],
        "draft_words": draftp[0],
        "draft_scales": draftp[1],
        "offs": striped8(idx),
        "offs2": striped8(idx2),
        "offs3": striped8(idx3),
        "offs4": striped8(idx4),
        "offs5": striped8(idx5),
    }


def reference(states, wq_words, wq_scales, cache_words, cache_scales, draft_words, draft_scales, offs, offs2, offs3, offs4, offs5):
    idx = unstriped8(offs)
    idx2 = unstriped8(offs2)
    idx3 = unstriped8(offs3)
    idx4 = unstriped8(offs4)
    idx5 = unstriped8(offs5)
    wqu = unpack_weight(wq_words, wq_scales, "e4m3")
    cacheu = unpack_weight(cache_words, cache_scales, "e2m1")
    draftu = unpack_weight(draft_words, draft_scales, "e4m3")
    statesq = mxq(f64(states), 0, "e4m3")
    qv = wqu.T @ statesq
    qvq = mxq(qv, 0, "e4m3")
    a = qvq.T @ cacheu
    b = statesq.T @ draftu
    nb = np.zeros((Q, U))
    nb[np.arange(Q)[:, None], idx2[np.arange(Q) % 128 // 16]] = pick8(b, idx, 16)
    w = np.maximum(pick8(nb, idx3, 16), pick8(a, idx4, 16))
    n2 = np.zeros((Q, U))
    n2[np.arange(Q)[:, None], idx5[np.arange(Q) % 128 // 16]] = w
    r = n2 - nb
    y = pick8(r, idx3, 16)
    return y

@@ -1,0 +1,153 @@
+from contextlib import ExitStack
+
+import concourse.mybir as mybir
+from concourse.masks import make_identity
+
+FLOPS = 335544320
+
+F32 = mybir.dt.float32
+BF16 = mybir.dt.bfloat16
+I32 = mybir.dt.int32
+U32 = mybir.dt.uint32
+U16 = mybir.dt.uint16
+U8 = mybir.dt.uint8
+FP8X4 = mybir.dt.float8_e4m3fn_x4
+FP4X4 = mybir.dt.float4_e2m1fn_x4
+COPY = mybir.ActivationFunctionType.Copy
+ALU = mybir.AluOpType
+
+P = 128
+Q = 128
+K = 512
+TOK = 1024
+SLOTS = 512
+HALF = SLOTS // 2
+PIECE = 256
+
+
+def load_scale_rows(nc, plane, scales):
+    rows = scales[0].bitcast(I32)
+    for r in range(4):
+        nc.sync.dma_start(plane[r:P:32, :].bitcast(I32), rows[r:16:4, :])
+
+
+def half(offsets, h):
+    return offsets[:, h * (HALF // 16) : (h + 1) * (HALF // 16)]
+
+
+def tile_attend_beamtwice_side_kernel(tc, states, wq_words, wq_scales, cache_words, cache_scales, draft_words, draft_scales, offs, offs2, offs3, offs4, offs5, out):
+    nc = tc.nc
+    with ExitStack() as ctx:
+        sb = ctx.enter_context(tc.tile_pool(name="sb", bufs=1))
+        ps = ctx.enter_context(tc.psum_pool(name="ps", bufs=1))
+
+        lst1 = sb.tile([P, SLOTS // 16], U16, name="lst1")
+        lst2 = sb.tile([P, SLOTS // 16], U16, name="lst2")
+        lst3 = sb.tile([P, SLOTS // 16], U16, name="lst3")
+        lst4 = sb.tile([P, SLOTS // 16], U16, name="lst4")
+        lst5 = sb.tile([P, SLOTS // 16], U16, name="lst5")
+
+        d_plane = sb.tile([P, TOK], U8, name="d_plane", align_bytes=256)
+        w_plane = sb.tile([P, K], U8, name="w_plane", align_bytes=256)
+        c_plane = sb.tile([P, TOK], U8, name="c_plane", align_bytes=256)
+        nb = sb.tile([P, TOK], F32, name="nb", align_bytes=256)
+        n2 = sb.tile([P, TOK], F32, name="n2", align_bytes=256)
+        nc.vector.memset(d_plane[:].bitcast(I32), 0)
+        nc.vector.memset(w_plane[:].bitcast(I32), 0)
+        nc.vector.memset(c_plane[:].bitcast(I32), 0)
+        nc.vector.memset(nb[:], 0.0)
+        nc.vector.memset(n2[:], 0.0)
+        ident = sb.tile([P, P], F32, name="ident", align_bytes=256)
+        make_identity(nc, ident[:])
+
+        raw = sb.tile([P, 4 * Q], F32, name="raw", align_bytes=256)
+        nc.sync.dma_start(raw[:], states.rearrange("(p t) q -> p (t q)", t=4))
+        load_scale_rows(nc, d_plane, draft_scales)
+        d_src = draft_words[0].rearrange("p n t -> p (n t)").bitcast(I32)
+        d_words = [sb.tile([P, TOK // 2], U32, name="d_words%d" % j, align_bytes=256) for j in range(2)]
+        for j in range(2):
+            nc.sync.dma_start(d_words[j][:].bitcast(I32), d_src[:, j * (TOK // 2) : (j + 1) * (TOK // 2)])
+        w_words = sb.tile([P, K], U32, name="w_words", align_bytes=256)
+        nc.sync.dma_start(w_words[:].bitcast(I32), wq_words[0].rearrange("p n t -> p (n t)").bitcast(I32))
+        nc.sync.dma_start(lst1[:], offs)
+        load_scale_rows(nc, w_plane, wq_scales)
+        nc.sync.dma_start(lst2[:], offs2)
+        c_words = sb.tile([P, 2 * TOK], U8, name="c_words", align_bytes=256)
+        nc.sync.dma_start(c_words[:].bitcast(I32), cache_words[0].bitcast(I32))
+        load_scale_rows(nc, c_plane, cache_scales)
+        nc.sync.dma_start(lst4[:], offs4)
+        nc.sync.dma_start(lst3[:], offs3)
+        nc.sync.dma_start(lst5[:], offs5)
+
+        s_bf = sb.tile([P, 4 * Q], BF16, name="s_bf", align_bytes=256)
+        nc.vector.tensor_copy(
+            s_bf[:].rearrange("p (c i t) -> p c t i", i=4, t=4),
+            raw[:].rearrange("p (t c i) -> p c t i", i=4, t=4),
+        )
+        s_codes = sb.tile([P, Q], U32, name="s_codes", align_bytes=256)
+        s_plane = sb.tile([P, Q], U8, name="s_plane", align_bytes=256)
+        nc.vector.quantize_mx(s_codes[:].bitcast(FP8X4), s_plane[:], s_bf[:])
+
+        b = sb.tile([P, TOK], F32, name="b", align_bytes=256)
+        for j in range(TOK // PIECE):
+            bank = ps.tile([P, PIECE], F32, name="score%d" % j)
+            cols = slice(j * PIECE, (j + 1) * PIECE)
+            wcols = slice((j % 2) * PIECE, (j % 2 + 1) * PIECE)
+            nc.tensor.matmul_mx(bank[:], lhsT=s_codes[:].bitcast(FP8X4), lhsT_scale=s_plane[:],
+                                rhs=d_words[j // 2][:, wcols].bitcast(FP8X4), rhs_scale=d_plane[:, cols], start=True, stop=True)
+            if j % 2 == 0:
+                nc.vector.tensor_copy(b[:, cols], bank[:])
+            else:
+                nc.scalar.activation(b[:, cols], bank[:], COPY)
+
+        qt = sb.tile([P, K], BF16, name="qt", align_bytes=256)
+        qt_dealt = qt[:].rearrange("q (u p e) -> q u p e", u=2, e=2)
+        for j in range(K // PIECE):
+            qbank = ps.tile([P, PIECE], F32, name="query%d" % j)
+            cols = slice(j * PIECE, (j + 1) * PIECE)
+            nc.tensor.matmul_mx(qbank[:], lhsT=s_codes[:].bitcast(FP8X4), lhsT_scale=s_plane[:],
+                                rhs=w_words[:, cols].bitcast(FP8X4), rhs_scale=w_plane[:, cols], start=True, stop=True)
+            nc.scalar.activation(qt_dealt[:, :, j * 64 : (j + 1) * 64, :], qbank[:].rearrange("q (p u e) -> q u p e", u=2, e=2), COPY)
+
+        picked = [sb.tile([P, HALF], F32, name="picked%d" % h, align_bytes=256) for h in range(2)]
+        for h in range(2):
+            nc.vector.tensor_copy(picked[h][:], b[:].indirect(half(lst1, h)))
+        for h in range(2):
+            nc.scalar.activation(nb[:].indirect(half(lst2, h)), picked[h][:], COPY)
+
+        turned = ps.tile([P, 2, Q], F32, name="turned")
+        qt_words = qt[:].bitcast(F32)
+        for u in range(2):
+            nc.tensor.transpose(turned[:, u, :], qt_words[:, u * P : (u + 1) * P], ident[:])
+        q_bf = sb.tile([P, 4 * Q], BF16, name="q_bf", align_bytes=256)
+        nc.vector.tensor_copy(q_bf[:].bitcast(F32).rearrange("p (q u) -> p q u", u=2), turned[:].rearrange("p u q -> p q u"))
+        q_codes = sb.tile([P, Q], U32, name="q_codes", align_bytes=256)
+        q_plane = sb.tile([P, Q], U8, name="q_plane", align_bytes=256)
+        nc.vector.quantize_mx(q_codes[:].bitcast(FP8X4), q_plane[:], q_bf[:])
+
+        a = sb.tile([P, TOK], F32, name="a", align_bytes=256)
+        for j in range(TOK // PIECE):
+            bank = ps.tile([P, PIECE], F32, name="score%d" % j)
+            cols = slice(j * PIECE, (j + 1) * PIECE)
+            nc.tensor.matmul_mx(bank[:], lhsT=q_codes[:].bitcast(FP8X4), lhsT_scale=q_plane[:],
+                                rhs=c_words[:, 2 * j * PIECE : 2 * (j + 1) * PIECE].bitcast(FP4X4), rhs_scale=c_plane[:, cols], start=True, stop=True)
+            nc.vector.tensor_copy(a[:, cols], bank[:])
+
+        a_picked = [sb.tile([P, HALF], F32, name="a_picked%d" % h, align_bytes=256) for h in range(2)]
+        nb_picked = [sb.tile([P, HALF], F32, name="nb_picked%d" % h, align_bytes=256) for h in range(2)]
+        w = [sb.tile([P, HALF], F32, name="w%d" % h, align_bytes=256) for h in range(2)]
+        for h in range(2):
+            nc.scalar.activation(nb_picked[h][:], nb[:].indirect(half(lst3, h)), COPY)
+        for h in range(2):
+            nc.vector.tensor_copy(a_picked[h][:], a[:].indirect(half(lst4, h)))
+            nc.vector.tensor_tensor(w[h][:], nb_picked[h][:], a_picked[h][:], ALU.max)
+        for h in range(2):
+            nc.scalar.activation(n2[:].indirect(half(lst5, h)), w[h][:], COPY)
+
+        r = sb.tile([P, TOK], F32, name="r", align_bytes=256)
+        nc.vector.tensor_tensor(r[:], n2[:], nb[:], ALU.subtract)
+        y = [sb.tile([P, HALF], F32, name="y%d" % h, align_bytes=256) for h in range(2)]
+        nc.vector.tensor_copy(y[0][:], r[:].indirect(half(lst3, 0)))
+        nc.scalar.activation(y[1][:], r[:].indirect(half(lst3, 1)), COPY)
+        nc.sync.dma_start(out[:, 0:HALF], y[0][:])
+        nc.scalar.dma_start(out[:, HALF:SLOTS], y[1][:])

@@ -1,7 +1,6 @@
 from contextlib import ExitStack
 
 import concourse.mybir as mybir
-from concourse.masks import make_identity
 
 FLOPS = 335544320
 
@@ -23,12 +22,11 @@ TOK = 1024
 SLOTS = 512
 HALF = SLOTS // 2
 PIECE = 256
+B_WIDTHS = (256, 256, 256, 128, 128)
 
 
-def load_scale_rows(nc, plane, scales):
-    rows = scales[0].bitcast(I32)
-    for r in range(4):
-        nc.sync.dma_start(plane[r:P:32, :].bitcast(I32), rows[r:16:4, :])
+def load_scale_rows(nc, plane, scales, j):
+    nc.sync.dma_start(plane[j:P:32, :].bitcast(I32), scales[0].bitcast(I32)[j:16:4, :])
 
 
 def half(offsets, h):
@@ -48,33 +46,36 @@ def tile_attend_beamtwice_side_kernel(tc, states, wq_words, wq_scales, cache_wor
         lst5 = sb.tile([P, SLOTS // 16], U16, name="lst5")
 
         d_plane = sb.tile([P, TOK], U8, name="d_plane", align_bytes=256)
-        w_plane = sb.tile([P, K], U8, name="w_plane", align_bytes=256)
+        w_plane = sb.tile([P, 4 * K], U8, name="w_plane", align_bytes=256)
         c_plane = sb.tile([P, TOK], U8, name="c_plane", align_bytes=256)
         nb = sb.tile([P, TOK], F32, name="nb", align_bytes=256)
         n2 = sb.tile([P, TOK], F32, name="n2", align_bytes=256)
         nc.vector.memset(d_plane[:].bitcast(I32), 0)
-        nc.vector.memset(w_plane[:].bitcast(I32), 0)
+        nc.vector.memset(w_plane[:, 0:K].bitcast(I32), 0)
         nc.vector.memset(c_plane[:].bitcast(I32), 0)
         nc.vector.memset(nb[:], 0.0)
         nc.vector.memset(n2[:], 0.0)
-        ident = sb.tile([P, P], F32, name="ident", align_bytes=256)
-        make_identity(nc, ident[:])
 
         raw = sb.tile([P, 4 * Q], F32, name="raw", align_bytes=256)
-        nc.sync.dma_start(raw[:], states.rearrange("(p t) q -> p (t q)", t=4))
-        load_scale_rows(nc, d_plane, draft_scales)
         d_src = draft_words[0].rearrange("p n t -> p (n t)").bitcast(I32)
         d_words = [sb.tile([P, TOK // 2], U32, name="d_words%d" % j, align_bytes=256) for j in range(2)]
-        for j in range(2):
-            nc.sync.dma_start(d_words[j][:].bitcast(I32), d_src[:, j * (TOK // 2) : (j + 1) * (TOK // 2)])
+        w_rows = w_plane[:].bitcast(I32)
         w_words = sb.tile([P, K], U32, name="w_words", align_bytes=256)
+        c_words = sb.tile([P, 2 * TOK], U8, name="c_words", align_bytes=256)
+        nc.sync.dma_start(raw[:], states.rearrange("(p t) q -> p (t q)", t=4))
+        nc.sync.dma_start(d_words[0][:].bitcast(I32), d_src[:, 0 : TOK // 2])
+        load_scale_rows(nc, d_plane, draft_scales, 0)
+        nc.sync.dma_start(w_rows[0:4, :].rearrange("j (g n) -> j g n", g=4), wq_scales[0].bitcast(I32).rearrange("(g j) n -> j g n", j=4))
+        for j in range(1, 4):
+            load_scale_rows(nc, d_plane, draft_scales, j)
+        nc.sync.dma_start(d_words[1][:].bitcast(I32), d_src[:, TOK // 2 : TOK])
         nc.sync.dma_start(w_words[:].bitcast(I32), wq_words[0].rearrange("p n t -> p (n t)").bitcast(I32))
         nc.sync.dma_start(lst1[:], offs)
-        load_scale_rows(nc, w_plane, wq_scales)
-        nc.sync.dma_start(lst2[:], offs2)
-        c_words = sb.tile([P, 2 * TOK], U8, name="c_words", align_bytes=256)
         nc.sync.dma_start(c_words[:].bitcast(I32), cache_words[0].bitcast(I32))
-        load_scale_rows(nc, c_plane, cache_scales)
+        load_scale_rows(nc, c_plane, cache_scales, 0)
+        nc.sync.dma_start(lst2[:], offs2)
+        for j in range(1, 4):
+            load_scale_rows(nc, c_plane, cache_scales, j)
         nc.sync.dma_start(lst4[:], offs4)
         nc.sync.dma_start(lst3[:], offs3)
         nc.sync.dma_start(lst5[:], offs5)
@@ -88,39 +89,44 @@ def tile_attend_beamtwice_side_kernel(tc, states, wq_words, wq_scales, cache_wor
         s_plane = sb.tile([P, Q], U8, name="s_plane", align_bytes=256)
         nc.vector.quantize_mx(s_codes[:].bitcast(FP8X4), s_plane[:], s_bf[:])
 
+        for g in range(1, 4):
+            nc.vector.tensor_copy(w_rows[32 * g : 32 * g + 4, 0 : K // 4], w_rows[0:4, g * (K // 4) : (g + 1) * (K // 4)])
+
+        w_plane_dealt = sb.tile([P, K], U8, name="w_plane_dealt", align_bytes=256)
+        nc.vector.tensor_copy(w_plane_dealt[:].rearrange("p (t m) -> p t m", t=4), w_plane[:, 0:K].rearrange("p (m t) -> p t m", t=4))
+
         b = sb.tile([P, TOK], F32, name="b", align_bytes=256)
-        for j in range(TOK // PIECE):
+        start = 0
+        for j, width in enumerate(B_WIDTHS):
             bank = ps.tile([P, PIECE], F32, name="score%d" % j)
-            cols = slice(j * PIECE, (j + 1) * PIECE)
-            wcols = slice((j % 2) * PIECE, (j % 2 + 1) * PIECE)
-            nc.tensor.matmul_mx(bank[:], lhsT=s_codes[:].bitcast(FP8X4), lhsT_scale=s_plane[:],
-                                rhs=d_words[j // 2][:, wcols].bitcast(FP8X4), rhs_scale=d_plane[:, cols], start=True, stop=True)
-            if j % 2 == 0:
-                nc.vector.tensor_copy(b[:, cols], bank[:])
+            cols = slice(start, start + width)
+            wcols = slice(start % (TOK // 2), start % (TOK // 2) + width)
+            nc.tensor.matmul_mx(bank[:, 0:width], lhsT=s_codes[:].bitcast(FP8X4), lhsT_scale=s_plane[:],
+                                rhs=d_words[start // (TOK // 2)][:, wcols].bitcast(FP8X4), rhs_scale=d_plane[:, cols], start=True, stop=True)
+            if j % 2 == 1:
+                nc.vector.tensor_copy(b[:, cols], bank[:, 0:width])
             else:
-                nc.scalar.activation(b[:, cols], bank[:], COPY)
+                nc.scalar.activation(b[:, cols], bank[:, 0:width], COPY)
+            start += width
 
-        qt = sb.tile([P, K], BF16, name="qt", align_bytes=256)
-        qt_dealt = qt[:].rearrange("q (u p e) -> q u p e", u=2, e=2)
-        for j in range(K // PIECE):
-            qbank = ps.tile([P, PIECE], F32, name="query%d" % j)
-            cols = slice(j * PIECE, (j + 1) * PIECE)
-            nc.tensor.matmul_mx(qbank[:], lhsT=s_codes[:].bitcast(FP8X4), lhsT_scale=s_plane[:],
-                                rhs=w_words[:, cols].bitcast(FP8X4), rhs_scale=w_plane[:, cols], start=True, stop=True)
-            nc.scalar.activation(qt_dealt[:, :, j * 64 : (j + 1) * 64, :], qbank[:].rearrange("q (p u e) -> q u p e", u=2, e=2), COPY)
+        w_dealt = sb.tile([P, K], U32, name="w_dealt", align_bytes=256)
+        nc.vector.tensor_copy(
+            w_dealt[:].rearrange("p (t c i) -> p c t i", t=4, i=4),
+            w_words[:].rearrange("p (c i t) -> p c t i", t=4, i=4),
+        )
 
-        picked = [sb.tile([P, HALF], F32, name="picked%d" % h, align_bytes=256) for h in range(2)]
-        for h in range(2):
-            nc.vector.tensor_copy(picked[h][:], b[:].indirect(half(lst1, h)))
-        for h in range(2):
-            nc.scalar.activation(nb[:].indirect(half(lst2, h)), picked[h][:], COPY)
+        picked = sb.tile([P, SLOTS], F32, name="picked", align_bytes=256)
+        nc.vector.tensor_copy(picked[:, 0:HALF], b[:].indirect(half(lst1, 0)))
+        nc.scalar.activation(picked[:, HALF:SLOTS], b[:].indirect(half(lst1, 1)), COPY)
+        nc.scalar.activation(nb[:].indirect(lst2[:]), picked[:], COPY)
 
-        turned = ps.tile([P, 2, Q], F32, name="turned")
-        qt_words = qt[:].bitcast(F32)
-        for u in range(2):
-            nc.tensor.transpose(turned[:, u, :], qt_words[:, u * P : (u + 1) * P], ident[:])
+        qbank = ps.tile([P, 4, Q], F32, name="score4")
+        for t in range(4):
+            cols = slice(t * P, (t + 1) * P)
+            nc.tensor.matmul_mx(qbank[:, t, :], lhsT=w_dealt[:, cols].bitcast(FP8X4), lhsT_scale=w_plane_dealt[:, cols],
+                                rhs=s_codes[:].bitcast(FP8X4), rhs_scale=s_plane[:], start=True, stop=True)
         q_bf = sb.tile([P, 4 * Q], BF16, name="q_bf", align_bytes=256)
-        nc.vector.tensor_copy(q_bf[:].bitcast(F32).rearrange("p (q u) -> p q u", u=2), turned[:].rearrange("p u q -> p q u"))
+        nc.vector.tensor_copy(q_bf[:].rearrange("p (q t) -> p q t", t=4), qbank[:].rearrange("p t q -> p q t"))
         q_codes = sb.tile([P, Q], U32, name="q_codes", align_bytes=256)
         q_plane = sb.tile([P, Q], U8, name="q_plane", align_bytes=256)
         nc.vector.quantize_mx(q_codes[:].bitcast(FP8X4), q_plane[:], q_bf[:])
@@ -133,14 +139,14 @@ def tile_attend_beamtwice_side_kernel(tc, states, wq_words, wq_scales, cache_wor
                                 rhs=c_words[:, 2 * j * PIECE : 2 * (j + 1) * PIECE].bitcast(FP4X4), rhs_scale=c_plane[:, cols], start=True, stop=True)
             nc.vector.tensor_copy(a[:, cols], bank[:])
 
-        a_picked = [sb.tile([P, HALF], F32, name="a_picked%d" % h, align_bytes=256) for h in range(2)]
         nb_picked = [sb.tile([P, HALF], F32, name="nb_picked%d" % h, align_bytes=256) for h in range(2)]
         w = [sb.tile([P, HALF], F32, name="w%d" % h, align_bytes=256) for h in range(2)]
         for h in range(2):
             nc.scalar.activation(nb_picked[h][:], nb[:].indirect(half(lst3, h)), COPY)
         for h in range(2):
-            nc.vector.tensor_copy(a_picked[h][:], a[:].indirect(half(lst4, h)))
-            nc.vector.tensor_tensor(w[h][:], nb_picked[h][:], a_picked[h][:], ALU.max)
+            a_picked = sb.tile([P, HALF], F32, name="a_picked", align_bytes=256)
+            nc.vector.tensor_copy(a_picked[:], a[:].indirect(half(lst4, h)))
+            nc.vector.tensor_tensor(w[h][:], nb_picked[h][:], a_picked[:], ALU.max)
         for h in range(2):
             nc.scalar.activation(n2[:].indirect(half(lst5, h)), w[h][:], COPY)
 

@@ -1,6 +1,7 @@
 from contextlib import ExitStack
 
 import concourse.mybir as mybir
+from concourse.masks import make_identity
 
 FLOPS = 335544320
 
@@ -22,6 +23,8 @@ TOK = 1024
 SLOTS = 512
 HALF = SLOTS // 2
 PIECE = 256
+LEAD = 96
+VEC_COLS = 768
 B_WIDTHS = (256, 256, 256, 128, 128)
 
 
@@ -55,6 +58,9 @@ def tile_attend_beamtwice_side_kernel(tc, states, wq_words, wq_scales, cache_wor
         nc.vector.memset(c_plane[:].bitcast(I32), 0)
         nc.vector.memset(nb[:], 0.0)
         nc.vector.memset(n2[:], 0.0)
+
+        ident = sb.tile([P, P], F32, name="ident", align_bytes=256)
+        make_identity(nc, ident[:])
 
         raw = sb.tile([P, 4 * Q], F32, name="raw", align_bytes=256)
         d_src = draft_words[0].rearrange("p n t -> p (n t)").bitcast(I32)
@@ -139,19 +145,32 @@ def tile_attend_beamtwice_side_kernel(tc, states, wq_words, wq_scales, cache_wor
                                 rhs=c_words[:, 2 * j * PIECE : 2 * (j + 1) * PIECE].bitcast(FP4X4), rhs_scale=c_plane[:, cols], start=True, stop=True)
             nc.vector.tensor_copy(a[:, cols], bank[:])
 
-        nb_picked = [sb.tile([P, HALF], F32, name="nb_picked%d" % h, align_bytes=256) for h in range(2)]
-        w = [sb.tile([P, HALF], F32, name="w%d" % h, align_bytes=256) for h in range(2)]
+        a_picked = sb.tile([P, SLOTS], F32, name="a_picked", tag="a_picked", align_bytes=256)
+        nb_picked = sb.tile([P, SLOTS], F32, name="nb_picked", align_bytes=256)
+        w = sb.tile([P, SLOTS], F32, name="w", align_bytes=256)
         for h in range(2):
-            nc.scalar.activation(nb_picked[h][:], nb[:].indirect(half(lst3, h)), COPY)
-        for h in range(2):
-            a_picked = sb.tile([P, HALF], F32, name="a_picked", align_bytes=256)
-            nc.vector.tensor_copy(a_picked[:], a[:].indirect(half(lst4, h)))
-            nc.vector.tensor_tensor(w[h][:], nb_picked[h][:], a_picked[:], ALU.max)
-        for h in range(2):
-            nc.scalar.activation(n2[:].indirect(half(lst5, h)), w[h][:], COPY)
+            cols = slice(h * HALF, (h + 1) * HALF)
+            nc.scalar.activation(nb_picked[:, cols], nb[:].indirect(half(lst3, h)), COPY)
+            nc.vector.tensor_copy(a_picked[:, cols], a[:].indirect(half(lst4, h)))
+        for lo, hi in ((0, LEAD), (LEAD, HALF), (HALF, SLOTS)):
+            nc.vector.tensor_tensor(w[:, lo:hi], nb_picked[:, lo:hi], a_picked[:, lo:hi], ALU.max)
+        for lo, hi in ((0, LEAD), (LEAD, SLOTS)):
+            nc.scalar.activation(n2[:].indirect(lst5[:, lo // 16 : hi // 16]), w[:, lo:hi], COPY)
 
+        nb_turned = sb.tile([P, VEC_COLS], F32, name="nb_turned", tag="a_picked", align_bytes=256)
+        spans = ((0, 512), (512, VEC_COLS))
+        for j, (lo, hi) in enumerate(spans):
+            bank = ps.tile([P, hi - lo], F32, name="score%d" % j)
+            for c in range(lo, hi, P):
+                nc.tensor.transpose(bank[:, c - lo : c - lo + P], nb[:, c : c + P], ident[:])
+            nc.vector.tensor_copy(nb_turned[:, lo:hi], bank[:])
         r = sb.tile([P, TOK], F32, name="r", align_bytes=256)
-        nc.vector.tensor_tensor(r[:], n2[:], nb[:], ALU.subtract)
+        for j, (lo, hi) in enumerate(spans):
+            bank = ps.tile([P, hi - lo], F32, name="score%d" % (2 + j))
+            for c in range(lo, hi, P):
+                nc.tensor.transpose(bank[:, c - lo : c - lo + P], nb_turned[:, c : c + P], ident[:])
+            nc.vector.tensor_tensor(r[:, lo:hi], n2[:, lo:hi], bank[:], ALU.subtract)
+        nc.gpsimd.tensor_tensor(r[:, VEC_COLS:TOK], n2[:, VEC_COLS:TOK], nb[:, VEC_COLS:TOK], ALU.subtract)
         y = [sb.tile([P, HALF], F32, name="y%d" % h, align_bytes=256) for h in range(2)]
         nc.vector.tensor_copy(y[0][:], r[:].indirect(half(lst3, 0)))
         nc.scalar.activation(y[1][:], r[:].indirect(half(lst3, 1)), COPY)

from contextlib import ExitStack

import concourse.mybir as mybir
from concourse.masks import make_identity

FLOPS = 335544320

F32 = mybir.dt.float32
BF16 = mybir.dt.bfloat16
I32 = mybir.dt.int32
U32 = mybir.dt.uint32
U16 = mybir.dt.uint16
U8 = mybir.dt.uint8
FP8X4 = mybir.dt.float8_e4m3fn_x4
FP4X4 = mybir.dt.float4_e2m1fn_x4
COPY = mybir.ActivationFunctionType.Copy
ALU = mybir.AluOpType

P = 128
Q = 128
K = 512
TOK = 1024
SLOTS = 512
HALF = SLOTS // 2
PIECE = 256
LEAD = 96
VEC_COLS = 768
B_WIDTHS = (256, 256, 256, 128, 128)


def load_scale_rows(nc, plane, scales, j):
    nc.sync.dma_start(plane[j:P:32, :].bitcast(I32), scales[0].bitcast(I32)[j:16:4, :])


def half(offsets, h):
    return offsets[:, h * (HALF // 16) : (h + 1) * (HALF // 16)]


def tile_attend_beamtwice_side_kernel(tc, states, wq_words, wq_scales, cache_words, cache_scales, draft_words, draft_scales, offs, offs2, offs3, offs4, offs5, out):
    nc = tc.nc
    with ExitStack() as ctx:
        sb = ctx.enter_context(tc.tile_pool(name="sb", bufs=1))
        ps = ctx.enter_context(tc.psum_pool(name="ps", bufs=1))

        lst1 = sb.tile([P, SLOTS // 16], U16, name="lst1")
        lst2 = sb.tile([P, SLOTS // 16], U16, name="lst2")
        lst3 = sb.tile([P, SLOTS // 16], U16, name="lst3")
        lst4 = sb.tile([P, SLOTS // 16], U16, name="lst4")
        lst5 = sb.tile([P, SLOTS // 16], U16, name="lst5")

        d_plane = sb.tile([P, TOK], U8, name="d_plane", align_bytes=256)
        w_plane = sb.tile([P, 4 * K], U8, name="w_plane", align_bytes=256)
        c_plane = sb.tile([P, TOK], U8, name="c_plane", align_bytes=256)
        nb = sb.tile([P, TOK], F32, name="nb", align_bytes=256)
        n2 = sb.tile([P, TOK], F32, name="n2", align_bytes=256)
        nc.vector.memset(d_plane[:].bitcast(I32), 0)
        nc.vector.memset(w_plane[:, 0:K].bitcast(I32), 0)
        nc.vector.memset(c_plane[:].bitcast(I32), 0)
        nc.vector.memset(nb[:], 0.0)
        nc.vector.memset(n2[:], 0.0)

        ident = sb.tile([P, P], F32, name="ident", align_bytes=256)
        make_identity(nc, ident[:])

        raw = sb.tile([P, 4 * Q], F32, name="raw", align_bytes=256)
        d_src = draft_words[0].rearrange("p n t -> p (n t)").bitcast(I32)
        d_words = [sb.tile([P, TOK // 2], U32, name="d_words%d" % j, align_bytes=256) for j in range(2)]
        w_rows = w_plane[:].bitcast(I32)
        w_words = sb.tile([P, K], U32, name="w_words", align_bytes=256)
        c_words = sb.tile([P, 2 * TOK], U8, name="c_words", align_bytes=256)
        nc.sync.dma_start(raw[:], states.rearrange("(p t) q -> p (t q)", t=4))
        nc.sync.dma_start(d_words[0][:].bitcast(I32), d_src[:, 0 : TOK // 2])
        load_scale_rows(nc, d_plane, draft_scales, 0)
        nc.sync.dma_start(w_rows[0:4, :].rearrange("j (g n) -> j g n", g=4), wq_scales[0].bitcast(I32).rearrange("(g j) n -> j g n", j=4))
        for j in range(1, 4):
            load_scale_rows(nc, d_plane, draft_scales, j)
        nc.sync.dma_start(d_words[1][:].bitcast(I32), d_src[:, TOK // 2 : TOK])
        nc.sync.dma_start(w_words[:].bitcast(I32), wq_words[0].rearrange("p n t -> p (n t)").bitcast(I32))
        nc.sync.dma_start(lst1[:], offs)
        nc.sync.dma_start(c_words[:].bitcast(I32), cache_words[0].bitcast(I32))
        load_scale_rows(nc, c_plane, cache_scales, 0)
        nc.sync.dma_start(lst2[:], offs2)
        for j in range(1, 4):
            load_scale_rows(nc, c_plane, cache_scales, j)
        nc.sync.dma_start(lst4[:], offs4)
        nc.sync.dma_start(lst3[:], offs3)
        nc.sync.dma_start(lst5[:], offs5)

        s_bf = sb.tile([P, 4 * Q], BF16, name="s_bf", align_bytes=256)
        nc.vector.tensor_copy(
            s_bf[:].rearrange("p (c i t) -> p c t i", i=4, t=4),
            raw[:].rearrange("p (t c i) -> p c t i", i=4, t=4),
        )
        s_codes = sb.tile([P, Q], U32, name="s_codes", align_bytes=256)
        s_plane = sb.tile([P, Q], U8, name="s_plane", align_bytes=256)
        nc.vector.quantize_mx(s_codes[:].bitcast(FP8X4), s_plane[:], s_bf[:])

        for g in range(1, 4):
            nc.vector.tensor_copy(w_rows[32 * g : 32 * g + 4, 0 : K // 4], w_rows[0:4, g * (K // 4) : (g + 1) * (K // 4)])

        w_plane_dealt = sb.tile([P, K], U8, name="w_plane_dealt", align_bytes=256)
        nc.vector.tensor_copy(w_plane_dealt[:].rearrange("p (t m) -> p t m", t=4), w_plane[:, 0:K].rearrange("p (m t) -> p t m", t=4))

        b = sb.tile([P, TOK], F32, name="b", align_bytes=256)
        start = 0
        for j, width in enumerate(B_WIDTHS):
            bank = ps.tile([P, PIECE], F32, name="score%d" % j)
            cols = slice(start, start + width)
            wcols = slice(start % (TOK // 2), start % (TOK // 2) + width)
            nc.tensor.matmul_mx(bank[:, 0:width], lhsT=s_codes[:].bitcast(FP8X4), lhsT_scale=s_plane[:],
                                rhs=d_words[start // (TOK // 2)][:, wcols].bitcast(FP8X4), rhs_scale=d_plane[:, cols], start=True, stop=True)
            if j % 2 == 1:
                nc.vector.tensor_copy(b[:, cols], bank[:, 0:width])
            else:
                nc.scalar.activation(b[:, cols], bank[:, 0:width], COPY)
            start += width

        w_dealt = sb.tile([P, K], U32, name="w_dealt", align_bytes=256)
        nc.vector.tensor_copy(
            w_dealt[:].rearrange("p (t c i) -> p c t i", t=4, i=4),
            w_words[:].rearrange("p (c i t) -> p c t i", t=4, i=4),
        )

        picked = sb.tile([P, SLOTS], F32, name="picked", align_bytes=256)
        nc.vector.tensor_copy(picked[:, 0:HALF], b[:].indirect(half(lst1, 0)))
        nc.scalar.activation(picked[:, HALF:SLOTS], b[:].indirect(half(lst1, 1)), COPY)
        nc.scalar.activation(nb[:].indirect(lst2[:]), picked[:], COPY)

        qbank = ps.tile([P, 4, Q], F32, name="score4")
        for t in range(4):
            cols = slice(t * P, (t + 1) * P)
            nc.tensor.matmul_mx(qbank[:, t, :], lhsT=w_dealt[:, cols].bitcast(FP8X4), lhsT_scale=w_plane_dealt[:, cols],
                                rhs=s_codes[:].bitcast(FP8X4), rhs_scale=s_plane[:], start=True, stop=True)
        q_bf = sb.tile([P, 4 * Q], BF16, name="q_bf", align_bytes=256)
        nc.vector.tensor_copy(q_bf[:].rearrange("p (q t) -> p q t", t=4), qbank[:].rearrange("p t q -> p q t"))
        q_codes = sb.tile([P, Q], U32, name="q_codes", align_bytes=256)
        q_plane = sb.tile([P, Q], U8, name="q_plane", align_bytes=256)
        nc.vector.quantize_mx(q_codes[:].bitcast(FP8X4), q_plane[:], q_bf[:])

        a = sb.tile([P, TOK], F32, name="a", align_bytes=256)
        for j in range(TOK // PIECE):
            bank = ps.tile([P, PIECE], F32, name="score%d" % j)
            cols = slice(j * PIECE, (j + 1) * PIECE)
            nc.tensor.matmul_mx(bank[:], lhsT=q_codes[:].bitcast(FP8X4), lhsT_scale=q_plane[:],
                                rhs=c_words[:, 2 * j * PIECE : 2 * (j + 1) * PIECE].bitcast(FP4X4), rhs_scale=c_plane[:, cols], start=True, stop=True)
            nc.vector.tensor_copy(a[:, cols], bank[:])

        a_picked = sb.tile([P, SLOTS], F32, name="a_picked", tag="a_picked", align_bytes=256)
        nb_picked = sb.tile([P, SLOTS], F32, name="nb_picked", align_bytes=256)
        w = sb.tile([P, SLOTS], F32, name="w", align_bytes=256)
        for h in range(2):
            cols = slice(h * HALF, (h + 1) * HALF)
            nc.scalar.activation(nb_picked[:, cols], nb[:].indirect(half(lst3, h)), COPY)
            nc.vector.tensor_copy(a_picked[:, cols], a[:].indirect(half(lst4, h)))
        for lo, hi in ((0, LEAD), (LEAD, HALF), (HALF, SLOTS)):
            nc.vector.tensor_tensor(w[:, lo:hi], nb_picked[:, lo:hi], a_picked[:, lo:hi], ALU.max)
        for lo, hi in ((0, LEAD), (LEAD, SLOTS)):
            nc.scalar.activation(n2[:].indirect(lst5[:, lo // 16 : hi // 16]), w[:, lo:hi], COPY)

        nb_turned = sb.tile([P, VEC_COLS], F32, name="nb_turned", tag="a_picked", align_bytes=256)
        spans = ((0, 512), (512, VEC_COLS))
        for j, (lo, hi) in enumerate(spans):
            bank = ps.tile([P, hi - lo], F32, name="score%d" % j)
            for c in range(lo, hi, P):
                nc.tensor.transpose(bank[:, c - lo : c - lo + P], nb[:, c : c + P], ident[:])
            nc.vector.tensor_copy(nb_turned[:, lo:hi], bank[:])
        r = sb.tile([P, TOK], F32, name="r", align_bytes=256)
        for j, (lo, hi) in enumerate(spans):
            bank = ps.tile([P, hi - lo], F32, name="score%d" % (2 + j))
            for c in range(lo, hi, P):
                nc.tensor.transpose(bank[:, c - lo : c - lo + P], nb_turned[:, c : c + P], ident[:])
            nc.vector.tensor_tensor(r[:, lo:hi], n2[:, lo:hi], bank[:], ALU.subtract)
        nc.gpsimd.tensor_tensor(r[:, VEC_COLS:TOK], n2[:, VEC_COLS:TOK], nb[:, VEC_COLS:TOK], ALU.subtract)
        y = [sb.tile([P, HALF], F32, name="y%d" % h, align_bytes=256) for h in range(2)]
        nc.vector.tensor_copy(y[0][:], r[:].indirect(half(lst3, 0)))
        nc.scalar.activation(y[1][:], r[:].indirect(half(lst3, 1)), COPY)
        nc.sync.dma_start(out[:, 0:HALF], y[0][:])
        nc.scalar.dma_start(out[:, HALF:SLOTS], y[1][:])
